import numpy as np
CORES = [10,34,74,98]
N = 4
F = 32
BOUND = 2289.7
def setup_inputs(rng):
    gr = rng.standard_normal((1, 128, N * F), dtype=np.float32) + rng.standard_normal((N, 128, N * F), dtype=np.float32)
    return {"gr": gr}
def setup_inputs_big(rng):
    d = setup_inputs(rng)
    for k in ("gr",): d[k] = (d[k].astype(np.float32) * 1024.0).astype(d[k].dtype)
    return d
def setup_inputs_small(rng):
    d = setup_inputs(rng)
    for k in ("gr",): d[k] = (d[k].astype(np.float32) * (1 / 1024.0)).astype(d[k].dtype)
    return d
def setup_inputs_apart(rng):
    d = setup_inputs(rng)
    f = (10.0 ** rng.permutation(np.linspace(-1.5, 1.5, N))).astype(np.float32).reshape(N, 1, 1)
    for k in ("gr",): d[k] = (d[k].astype(np.float32) * f).astype(d[k].dtype)
    return d
def setup_inputs_far(rng):
    d = setup_inputs(rng)
    for k in ("gr",): d[k] = (d[k].astype(np.float32) * 16384.0).astype(d[k].dtype)
    return d
def setup_inputs_over(rng):
    d = setup_inputs(rng)
    f = np.float32(10.0 ** rng.uniform(1.5, 3.5)) * np.where(rng.random((1, 128, N * F)) < 0.5, 0.1, 1.0).astype(np.float32)
    for k in ("gr",): d[k] = (d[k].astype(np.float32) * f).astype(d[k].dtype)
    return d
def reference(gr):
    s = gr.astype(np.float64).sum(axis=0)
    nrm = np.sqrt((s ** 2).sum())
    s = s * min(1.0, BOUND / nrm)
    return {"y": np.stack([s[:, F * r:F * r + F] for r in range(N)]).astype(np.float32)}

from concourse.bass import DstId, RemoteDMATransfer
from concourse.mybir import AluOpType, ActivationFunctionType

N = 4
F = 32
W = N * F
SHIFT = 2.0 ** -50

SCRATCH = {
    "gall": ("sbuf", [128, N * W], "float32"),
    "ones": ("sbuf", [128, 128], "float32"),
    "s": ("sbuf", [128, W], "float32"),
    "junk": ("sbuf", [128, W], "float32"),
    "part": ("sbuf", [128, 1], "float32"),
    "f": ("sbuf", [128, 1], "float32"),
    "rf": ("sbuf", [128, 1], "float32"),
    "u": ("sbuf", [128, 1], "float32"),
    "sq": ("sbuf", [128, 1], "float32"),
    "rc": ("sbuf", [128, 1], "float32"),
    "spre": ("sbuf", [128, F], "float32"),
    "ysb": ("sbuf", [128, F], "float32"),
    "acc": ("psum", [128, 512], "float32"),
    "tot": ("psum", [128, 512], "float32"),
}
SEMAPHORES = ["ld", "st", "snt"] + ["arr%d" % i for i in range(N)] + [
    "c_ones", "c_f", "c_rf", "c_a0", "c_a1", "c_a2", "c_s", "c_p", "c_pre", "c_t", "c_u", "c_q", "c_rc", "c_y"]


def rank_program(g, core, T, topo):
    r = T.rank_of(core)
    if r is None:
        return
    S = T.sem
    bound = float(T.tables["BOUND"])
    add, mult, vmax = AluOpType.add, AluOpType.mult, AluOpType.max
    Act = ActivationFunctionType

    def slot(i):
        return T.gall[:, W * i:W * (i + 1)]

    outs = [T.cores[(r + k) % N] for k in range(1, N)]
    ins = [(r - k) % N for k in range(1, N)]

    g.sync.dma_start(slot(r), T.gr[:]).then_inc(S.ld, 16)

    mask = -1
    for d in outs:
        if not topo.may_write(core, d):
            raise ValueError("rank core %d may not write to rank core %d" % (core, d))
        mask &= topo.mask(core, d)
    engines = bin(mask).count("1")
    ids = []
    for d in outs:
        rid, pid, _se = topo.addr(d)
        ids.append(DstId(rid=rid, pnc=pid))
    g.wait_ge(S.ld, 16)
    g.remote_dma_fused(
        [RemoteDMATransfer(dst_ids=ids, dma_engine_mask=mask, remote_sem=S["arr%d" % r],
                           srcs=[slot(r)], dsts=[slot(r) for _ in outs], alu_op=0)],
        local_sem=S.snt)

    g.vector.memset(T.ones[:], 1.0).then_inc(S.c_ones, 1)
    g.scalar.wait_ge(S.c_ones, 1)
    g.scalar.activation(T.f[:], T.ones[:, 0:1], Act.Sqrt, scale=SHIFT).then_inc(S.c_f, 1)

    acc = T.acc[:, 0:W]
    g.vector.wait_ge(S.ld, 16)
    g.vector.tensor_copy(acc, slot(r)).then_inc(S.c_a0, 1)
    g.vector.wait_ge(S.c_f, 1)
    g.vector.reciprocal(T.rf[:], T.f[:]).then_inc(S.c_rf, 1)
    g.vector.wait_ge(S.c_a0, 1)
    g.vector.wait_ge(S["arr%d" % ins[0]], engines)
    g.vector.tensor_tensor(acc, acc, slot(ins[0]), add).then_inc(S.c_a1, 1)
    g.vector.wait_ge(S.c_a1, 1)
    g.vector.wait_ge(S["arr%d" % ins[1]], engines)
    g.vector.tensor_tensor(acc, acc, slot(ins[1]), add).then_inc(S.c_a2, 1)
    g.vector.wait_ge(S.c_a2, 1)
    g.vector.wait_ge(S["arr%d" % ins[2]], engines)
    g.vector.tensor_tensor(T.s[:], acc, slot(ins[2]), add).then_inc(S.c_s, 1)

    g.scalar.wait_ge(S.c_s, 1)
    g.scalar.activation(T.junk[:], T.s[:], Act.Square, scale=1.0 / bound, accum_out=T.part[:]).then_inc(S.c_p, 1)
    g.vector.wait_ge(S.c_s, 1)
    g.vector.wait_ge(S.c_rf, 1)
    g.vector.tensor_scalar(T.spre[:], T.s[:, F * r:F * (r + 1)], T.rf[:], None, mult).then_inc(S.c_pre, 1)

    g.tensor.wait_ge(S.c_ones, 1)
    g.tensor.wait_ge(S.c_p, 1)
    g.tensor.matmul(T.tot[:, 0:1], T.ones[:], T.part[:], True, True).then_inc(S.c_t, 1)

    g.vector.wait_ge(S.c_t, 1)
    g.vector.tensor_scalar(T.u[:], T.tot[:, 0:1], 1.0, None, vmax).then_inc(S.c_u, 1)
    g.scalar.wait_ge(S.c_u, 1)
    g.scalar.activation(T.sq[:], T.u[:], Act.Sqrt, scale=SHIFT).then_inc(S.c_q, 1)
    g.vector.wait_ge(S.c_u, 1)
    g.vector.reciprocal(T.rc[:], T.u[:]).then_inc(S.c_rc, 1)
    g.vector.wait_ge(S.c_rc, 1)
    g.vector.wait_ge(S.c_pre, 1)
    g.vector.wait_ge(S.c_q, 1)
    g.vector.tensor_scalar(T.ysb[:], T.spre[:], T.rc[:], T.sq[:], mult, mult).then_inc(S.c_y, 1)

    g.sync.wait_ge(S.c_y, 1)
    g.sync.dma_start(T.y[:], T.ysb[:]).then_inc(S.st, 16)
    g.sync.wait_ge(S.st, 16)

    g.wait_ge(S.snt, engines)
